import numpy as np
CORES = [0,9,18,27,36,45,54,63,64,73,82,91,100,109,118,127]
N = 16
def setup_inputs(rng):
    return {"x": rng.standard_normal((N, 128, 16), dtype=np.float32)}
def reference(x):
    s = x.sum(axis=0, dtype=np.float64).astype(x.dtype)
    b = 16 // N
    return {"y": np.stack([s[:, r * b:(r + 1) * b] for r in range(N)])}

@@ -1,0 +1,65 @@
+from concourse.bass import DstId, RemoteDMATransfer
+
+SCRATCH = {
+    "xd": ("dram", [128, 16], "float32"),
+    "land": ("dram", [8, 128, 16], "float32"),
+    "part": ("dram", [2, 128, 16], "float32"),
+    "res": ("sbuf", [128, 16], "float32"),
+}
+SEMAPHORES = ["ld", "sent", "arr", "par", "got", "fin"]
+
+
+def roles(rank_core):
+    chip, k = divmod(rank_core, 8)
+    base = (k // 4) * 4
+    h = base + 3 if k == base + 2 else base + 2
+    f = [b for b in (base + 3, base + 2, base + 1, base) if b != k and b != h][0]
+    return chip * 8 + h, chip * 8 + f
+
+
+def rank_program(g, core, T, topo):
+    sem = T.sem
+    chip = topo.chip(core)
+    rank_core = {}
+    for c in T.cores:
+        rank_core[topo.chip(c)] = c
+
+    def dst(c):
+        rid, pid, _se = topo.addr(c)
+        return DstId(rid=rid, pnc=pid)
+
+    my_rank_core = rank_core[chip]
+    h_core, f_core = roles(my_rank_core)
+    rank = T.rank_of(core)
+
+    if rank is not None:
+        g.sync.dma_start(T.xd[:], T.x[:]).then_inc(sem.ld, 16)
+        g.wait_ge(sem.ld, 16)
+        chips = [(chip + 2 * j) % 16 for j in range(1, 9)]
+        hs = [roles(rank_core[c])[0] for c in chips]
+        g.remote_dma_fused(
+            [RemoteDMATransfer(dst_ids=[dst(h) for h in hs], dma_engine_mask=0x00FF, remote_sem=sem.arr,
+                               srcs=[T.xd[:]], dsts=[T.land[chip // 2] for _h in hs], alu_op=0)],
+            local_sem=sem.sent)
+        g.sync.wait_ge(sem.got, 16)
+        g.sync.dma_start(T.y[:], T.res[:, rank:rank + 1]).then_inc(sem.fin, 16)
+        g.wait_ge(sem.sent, 8)
+        g.wait_ge(sem.fin, 16)
+    elif core == h_core:
+        g.wait_ge(sem.arr, 64)
+        srcs = [T.land[i] for i in range(8)]
+        mate_f = roles(rank_core[chip ^ 1])[1]
+        g.remote_dma_fused(
+            [RemoteDMATransfer(dst_ids=[dst(f_core)], dma_engine_mask=0xFF00, remote_sem=sem.par,
+                               srcs=srcs, dsts=[T.part[0]], alu_op=1),
+             RemoteDMATransfer(dst_ids=[dst(mate_f)], dma_engine_mask=0x00FF, remote_sem=sem.par,
+                               srcs=srcs, dsts=[T.part[1]], alu_op=1)],
+            local_sem=sem.sent)
+        g.wait_ge(sem.sent, 16)
+    elif core == f_core:
+        g.wait_ge(sem.par, 16)
+        g.remote_dma_fused(
+            [RemoteDMATransfer(dst_ids=[dst(my_rank_core)], dma_engine_mask=0xFFFF, remote_sem=sem.got,
+                               srcs=[T.part[0], T.part[1]], dsts=[T.res[:]], alu_op=1)],
+            local_sem=sem.sent)
+        g.wait_ge(sem.sent, 16)

@@ -1,10 +1,12 @@
 from concourse.bass import DstId, RemoteDMATransfer
 
+W = 8
+
 SCRATCH = {
-    "xd": ("dram", [128, 16], "float32"),
-    "land": ("dram", [8, 128, 16], "float32"),
-    "part": ("dram", [2, 128, 16], "float32"),
-    "res": ("sbuf", [128, 16], "float32"),
+    "xb": ("dram", [2, 128, W], "float32"),
+    "land": ("dram", [8, 128, W], "float32"),
+    "part": ("dram", [2, 128, W], "float32"),
+    "res": ("sbuf", [128, W], "float32"),
 }
 SEMAPHORES = ["ld", "sent", "arr", "par", "got", "fin"]
 
@@ -33,27 +35,32 @@ def rank_program(g, core, T, topo):
     rank = T.rank_of(core)
 
     if rank is not None:
-        g.sync.dma_start(T.xd[:], T.x[:]).then_inc(sem.ld, 16)
-        g.wait_ge(sem.ld, 16)
-        chips = [(chip + 2 * j) % 16 for j in range(1, 9)]
-        hs = [roles(rank_core[c])[0] for c in chips]
-        g.remote_dma_fused(
-            [RemoteDMATransfer(dst_ids=[dst(h) for h in hs], dma_engine_mask=0x00FF, remote_sem=sem.arr,
-                               srcs=[T.xd[:]], dsts=[T.land[chip // 2] for _h in hs], alu_op=0)],
-            local_sem=sem.sent)
+        g.sync.dma_start(T.xb[0], T.x[:, 0:W]).then_inc(sem.ld, 16)
+        g.scalar.dma_start(T.xb[1], T.x[:, W:2 * W]).then_inc(sem.ld, 16)
+        g.wait_ge(sem.ld, 32)
+        s = chip // 2
+        trs = []
+        for p in range(2):
+            shift = 0 if p == s // 4 else 2
+            chips = [p * W + 2 * ((s + j + shift) % 4) + chip % 2 for j in range(1, 5)]
+            hs = [roles(rank_core[c])[0] for c in chips]
+            trs.append(RemoteDMATransfer(dst_ids=[dst(h) for h in hs], dma_engine_mask=0x0F << (4 * p),
+                                         remote_sem=sem.arr, srcs=[T.xb[p]],
+                                         dsts=[T.land[s] for _h in hs], alu_op=0))
+        g.remote_dma_fused(trs, local_sem=sem.sent)
         g.sync.wait_ge(sem.got, 16)
-        g.sync.dma_start(T.y[:], T.res[:, rank:rank + 1]).then_inc(sem.fin, 16)
+        g.sync.dma_start(T.y[:], T.res[:, rank % W:rank % W + 1]).then_inc(sem.fin, 16)
         g.wait_ge(sem.sent, 8)
         g.wait_ge(sem.fin, 16)
     elif core == h_core:
-        g.wait_ge(sem.arr, 64)
+        g.wait_ge(sem.arr, 32)
         srcs = [T.land[i] for i in range(8)]
         mate_f = roles(rank_core[chip ^ 1])[1]
         g.remote_dma_fused(
-            [RemoteDMATransfer(dst_ids=[dst(f_core)], dma_engine_mask=0xFF00, remote_sem=sem.par,
-                               srcs=srcs, dsts=[T.part[0]], alu_op=1),
-             RemoteDMATransfer(dst_ids=[dst(mate_f)], dma_engine_mask=0x00FF, remote_sem=sem.par,
-                               srcs=srcs, dsts=[T.part[1]], alu_op=1)],
+            [RemoteDMATransfer(dst_ids=[dst(mate_f)], dma_engine_mask=0x00FF, remote_sem=sem.par,
+                               srcs=srcs, dsts=[T.part[1]], alu_op=1),
+             RemoteDMATransfer(dst_ids=[dst(f_core)], dma_engine_mask=0xFF00, remote_sem=sem.par,
+                               srcs=srcs, dsts=[T.part[0]], alu_op=1)],
             local_sem=sem.sent)
         g.wait_ge(sem.sent, 16)
     elif core == f_core:

from concourse.bass import DstId, RemoteDMATransfer

W = 8

SCRATCH = {
    "xb": ("dram", [2, 128, W], "float32"),
    "land": ("dram", [8, 128, W], "float32"),
    "part": ("dram", [2, 128, W], "float32"),
    "res": ("sbuf", [128, W], "float32"),
}
SEMAPHORES = ["ld", "sent", "arr", "par", "got", "fin"]


def roles(rank_core):
    chip, k = divmod(rank_core, 8)
    base = (k // 4) * 4
    h = base + 3 if k == base + 2 else base + 2
    f = [b for b in (base + 3, base + 2, base + 1, base) if b != k and b != h][0]
    return chip * 8 + h, chip * 8 + f


def rank_program(g, core, T, topo):
    sem = T.sem
    chip = topo.chip(core)
    rank_core = {}
    for c in T.cores:
        rank_core[topo.chip(c)] = c

    def dst(c):
        rid, pid, _se = topo.addr(c)
        return DstId(rid=rid, pnc=pid)

    my_rank_core = rank_core[chip]
    h_core, f_core = roles(my_rank_core)
    rank = T.rank_of(core)

    if rank is not None:
        g.sync.dma_start(T.xb[0], T.x[:, 0:W]).then_inc(sem.ld, 16)
        g.scalar.dma_start(T.xb[1], T.x[:, W:2 * W]).then_inc(sem.ld, 16)
        g.wait_ge(sem.ld, 32)
        s = chip // 2
        trs = []
        for p in range(2):
            shift = 0 if p == s // 4 else 2
            chips = [p * W + 2 * ((s + j + shift) % 4) + chip % 2 for j in range(1, 5)]
            hs = [roles(rank_core[c])[0] for c in chips]
            trs.append(RemoteDMATransfer(dst_ids=[dst(h) for h in hs], dma_engine_mask=0x0F << (4 * p),
                                         remote_sem=sem.arr, srcs=[T.xb[p]],
                                         dsts=[T.land[s] for _h in hs], alu_op=0))
        g.remote_dma_fused(trs, local_sem=sem.sent)
        g.sync.wait_ge(sem.got, 16)
        g.sync.dma_start(T.y[:], T.res[:, rank % W:rank % W + 1]).then_inc(sem.fin, 16)
        g.wait_ge(sem.sent, 8)
        g.wait_ge(sem.fin, 16)
    elif core == h_core:
        g.wait_ge(sem.arr, 32)
        srcs = [T.land[i] for i in range(8)]
        mate_f = roles(rank_core[chip ^ 1])[1]
        g.remote_dma_fused(
            [RemoteDMATransfer(dst_ids=[dst(mate_f)], dma_engine_mask=0x00FF, remote_sem=sem.par,
                               srcs=srcs, dsts=[T.part[1]], alu_op=1),
             RemoteDMATransfer(dst_ids=[dst(f_core)], dma_engine_mask=0xFF00, remote_sem=sem.par,
                               srcs=srcs, dsts=[T.part[0]], alu_op=1)],
            local_sem=sem.sent)
        g.wait_ge(sem.sent, 16)
    elif core == f_core:
        g.wait_ge(sem.par, 16)
        g.remote_dma_fused(
            [RemoteDMATransfer(dst_ids=[dst(my_rank_core)], dma_engine_mask=0xFFFF, remote_sem=sem.got,
                               srcs=[T.part[0], T.part[1]], dsts=[T.res[:]], alu_op=1)],
            local_sem=sem.sent)
        g.wait_ge(sem.sent, 16)
